import numpy as np
import ml_dtypes


def mxq(x, axis, fmt="e4m3"):
    dtype, down = {"e4m3": (ml_dtypes.float8_e4m3fn, 7), "e5m2": (ml_dtypes.float8_e5m2, 14)}[fmt]
    v = np.moveaxis(np.asarray(x, np.float32).astype(ml_dtypes.bfloat16).astype(np.float64), axis, -1)
    blocks = v.reshape(v.shape[:-1] + (-1, 32))
    amax = np.abs(blocks).max(-1, keepdims=True)
    byte = np.maximum(np.where(amax > 0, np.frexp(amax)[1] - 1 + 127, 0) - down, 1)
    scale = np.exp2(byte - 127.0)
    codes = (blocks / scale).astype(np.float32).astype(dtype).astype(np.float64)
    return np.moveaxis((codes * scale).reshape(v.shape), -1, axis)


WIDE = False


def mx_kscale(k):
    if not WIDE:
        return np.ones(k)
    levels = np.array([18, -18])
    if k % 512:
        return np.exp2(np.random.permutation(np.resize(levels, k // 32))).repeat(32)
    a = np.empty((k // 512, 16))
    for p in range(k // 512):
        a[p, :8] = np.random.permutation(np.resize(levels, 8))
        for g in range(8):
            far = levels[np.abs(levels - a[p, g]) >= 10]
            a[p, g + 8] = far[np.random.randint(len(far))]
    return np.exp2(a.ravel()).repeat(32)


def f64(x):
    return np.asarray(x).astype(np.float64)


def striped(idx):
    return np.tile(np.asarray(idx).reshape(-1, 16).T, (8, 1)).astype(np.uint16)


def unstriped(offs):
    return offs[:16].T.reshape(-1).astype(np.int64)


B, N, T, D, DV, NQ = 1, 512, 2048, 512, 512, 128


def setup_inputs():
    n = np.random.standard_normal
    idx = np.random.permutation(T)[:B * N]
    u = mx_kscale(B * N)
    ut = np.ones(T)
    ut[idx] = u
    w = np.exp(n((B, N, NQ)))
    w = w / w.sum(1, keepdims=True)
    return {
        "wT": (w * u.reshape(B, N, 1)).astype(np.float32),
        "vT": (n((DV, T)) / ut).astype(np.float32),
        "offs": striped(idx),
    }


def reference(wT, vT, offs):
    idx = unstriped(offs)
    pick = lambda x: x[:, idx].reshape(x.shape[0], B, N).transpose(1, 0, 2)
    return mxq(f64(wT), 1, "e5m2").transpose(0, 2, 1) @ mxq(pick(f64(vT)).transpose(0, 2, 1), 1, "e4m3")

@@ -1,0 +1,98 @@
+from contextlib import ExitStack
+
+import concourse.mybir as mybir
+from concourse.masks import make_identity
+
+N, T, DV, NQ = 512, 2048, 512, 128
+FLOPS = 2 * N * NQ * DV
+
+P = 128
+PACK = 4
+BLOCKS = DV // P
+
+F32 = mybir.dt.float32
+BF16 = mybir.dt.bfloat16
+U32 = mybir.dt.uint32
+U16 = mybir.dt.uint16
+U8 = mybir.dt.uint8
+E4M3X4 = mybir.dt.float8_e4m3fn_x4
+E5M2X4 = mybir.dt.float8_e5m2_x4
+
+
+def tile_attend_spmm_kernel(tc, wT, vT, offs, out):
+    nc = tc.nc
+    with ExitStack() as ctx:
+        hold = ctx.enter_context(tc.tile_pool(name="hold", bufs=1))
+        psum = ctx.enter_context(tc.psum_pool(name="psum", bufs=1))
+
+        ident = hold.tile([P, P], F32, name="ident")
+        make_identity(nc, ident[:])
+
+        offsets = hold.tile([P, N // 16], U16, name="offsets")
+        pool_v = [hold.tile([P, T], F32, name=f"pool_v{b}", align_bytes=64) for b in range(BLOCKS)]
+        w_raw = hold.tile([P, PACK, NQ], F32, name="w_raw", align_bytes=64)
+
+        nc.sync.dma_start(offsets[:], offs)
+        for b in range(BLOCKS):
+            nc.sync.dma_start(out=pool_v[b][:], in_=vT[b * P:(b + 1) * P, :])
+        nc.sync.dma_start(out=w_raw[:], in_=wT.flatten_outer_dims().rearrange("(p t) q -> p t q", t=PACK))
+
+        v_codes = hold.tile([P, DV], U32, name="v_codes", align_bytes=64)
+        v_scales = hold.tile([P, DV], U8, name="v_scales", align_bytes=64)
+        w_codes = hold.tile([P, NQ], U32, name="w_codes", align_bytes=64)
+        w_scales = hold.tile([P, NQ], U8, name="w_scales", align_bytes=64)
+
+        grouped = []
+
+        def gather(b):
+            picked = hold.tile([P, 2, P, 2], BF16, name=f"picked{b}", align_bytes=64)
+            nc.vector.tensor_copy(picked[:].rearrange("d u p e -> d p u e"), pool_v[b][:].indirect(offsets[:]))
+            words = picked[:].rearrange("d u p e -> d (u p e)").bitcast(F32)
+            turned = psum.tile([P, 2, P], F32, name=f"turned{b}")
+            for u in range(2):
+                nc.tensor.transpose(turned[:, u, :], words[:, u * P:(u + 1) * P], ident[:])
+            g = hold.tile([P, P, PACK], BF16, name=f"grouped{b}", align_bytes=64)
+            nc.scalar.copy(out=g[:].bitcast(F32), in_=turned[:].rearrange("p u r -> p r u"))
+            grouped.append(g)
+
+        def quantize(b):
+            cols = slice(b * P, (b + 1) * P)
+            nc.vector.quantize_mx(
+                out=v_codes[:, cols].bitcast(E4M3X4),
+                scales=v_scales[:, cols],
+                in_=grouped[b][:].rearrange("p r t -> p (r t)"),
+            )
+
+        gather(0)
+        for b in range(1, BLOCKS - 1):
+            gather(b)
+            quantize(b - 1)
+        w_grouped = hold.tile([P, NQ, PACK], BF16, name="w_grouped", align_bytes=64)
+        nc.scalar.copy(out=w_grouped[:], in_=w_raw[:].rearrange("p t q -> p q t"))
+        gather(BLOCKS - 1)
+        quantize(BLOCKS - 2)
+        nc.vector.quantize_mx(
+            out=w_codes[:].bitcast(E5M2X4),
+            scales=w_scales[:],
+            in_=w_grouped[:].rearrange("p q t -> p (q t)"),
+        )
+        quantize(BLOCKS - 1)
+
+        acc = psum.tile([NQ, DV], F32, name="acc")
+        nc.tensor.matmul_mx(
+            out=acc[:],
+            lhsT=w_codes[:].bitcast(E5M2X4),
+            lhsT_scale=w_scales[:],
+            rhs=v_codes[:].bitcast(E4M3X4),
+            rhs_scale=v_scales[:],
+            start=True,
+            stop=True,
+        )
+        result = out.flatten_outer_dims()
+        half = DV // 2
+        left = hold.tile([NQ, half], F32, name="left")
+        right = hold.tile([NQ, half], F32, name="right")
+        nc.vector.tensor_copy(left[:], acc[:, 0:half])
+        nc.sync.dma_start(out=result[:, 0:half], in_=left[:])
+        nc.scalar.copy(out=right[:], in_=acc[:, half:DV])
+        nc.scalar.dma_start(out=result[:, half:DV], in_=right[:])

@@ -29,12 +29,13 @@ def tile_attend_spmm_kernel(tc, wT, vT, offs, out):
         make_identity(nc, ident[:])
 
         offsets = hold.tile([P, N // 16], U16, name="offsets")
-        pool_v = [hold.tile([P, T], F32, name=f"pool_v{b}", align_bytes=64) for b in range(BLOCKS)]
+        pool_v = [hold.tile([P, T], F32, name=f"pool_v{b}", tag=f"pool{b}", align_bytes=64) for b in range(BLOCKS)]
         w_raw = hold.tile([P, PACK, NQ], F32, name="w_raw", align_bytes=64)
 
-        nc.sync.dma_start(offsets[:], offs)
         for b in range(BLOCKS):
             nc.sync.dma_start(out=pool_v[b][:], in_=vT[b * P:(b + 1) * P, :])
+            if b == 0:
+                nc.sync.dma_start(offsets[:], offs)
         nc.sync.dma_start(out=w_raw[:], in_=wT.flatten_outer_dims().rearrange("(p t) q -> p t q", t=PACK))
 
         v_codes = hold.tile([P, DV], U32, name="v_codes", align_bytes=64)
@@ -42,18 +43,21 @@ def tile_attend_spmm_kernel(tc, wT, vT, offs, out):
         w_codes = hold.tile([P, NQ], U32, name="w_codes", align_bytes=64)
         w_scales = hold.tile([P, NQ], U8, name="w_scales", align_bytes=64)
 
-        grouped = []
+        turned = {}
+        grouped = {}
 
         def gather(b):
             picked = hold.tile([P, 2, P, 2], BF16, name=f"picked{b}", align_bytes=64)
             nc.vector.tensor_copy(picked[:].rearrange("d u p e -> d p u e"), pool_v[b][:].indirect(offsets[:]))
             words = picked[:].rearrange("d u p e -> d (u p e)").bitcast(F32)
-            turned = psum.tile([P, 2, P], F32, name=f"turned{b}")
+            turned[b] = psum.tile([P, 2, P], F32, name=f"turned{b}")
             for u in range(2):
-                nc.tensor.transpose(turned[:, u, :], words[:, u * P:(u + 1) * P], ident[:])
-            g = hold.tile([P, P, PACK], BF16, name=f"grouped{b}", align_bytes=64)
-            nc.scalar.copy(out=g[:].bitcast(F32), in_=turned[:].rearrange("p u r -> p r u"))
-            grouped.append(g)
+                nc.tensor.transpose(turned[b][:, u, :], words[:, u * P:(u + 1) * P], ident[:])
+
+        def group(b):
+            g = hold.tile([P, P, PACK], BF16, name=f"grouped{b}", tag=f"pool{b + 1}", align_bytes=64)
+            nc.scalar.copy(out=g[:].bitcast(F32), in_=turned[b][:].rearrange("p u r -> p r u"))
+            grouped[b] = g
 
         def quantize(b):
             cols = slice(b * P, (b + 1) * P)
@@ -66,16 +70,19 @@ def tile_attend_spmm_kernel(tc, wT, vT, offs, out):
         gather(0)
         for b in range(1, BLOCKS - 1):
             gather(b)
+            group(b - 1)
             quantize(b - 1)
+        gather(BLOCKS - 1)
         w_grouped = hold.tile([P, NQ, PACK], BF16, name="w_grouped", align_bytes=64)
         nc.scalar.copy(out=w_grouped[:], in_=w_raw[:].rearrange("p t q -> p q t"))
-        gather(BLOCKS - 1)
+        group(BLOCKS - 2)
         quantize(BLOCKS - 2)
         nc.vector.quantize_mx(
             out=w_codes[:].bitcast(E5M2X4),
             scales=w_scales[:],
             in_=w_grouped[:].rearrange("p q t -> p (q t)"),
         )
+        group(BLOCKS - 1)
         quantize(BLOCKS - 1)
 
         acc = psum.tile([NQ, DV], F32, name="acc")

@@ -74,7 +74,10 @@ def tile_attend_spmm_kernel(tc, wT, vT, offs, out):
             quantize(b - 1)
         gather(BLOCKS - 1)
         w_grouped = hold.tile([P, NQ, PACK], BF16, name="w_grouped", align_bytes=64)
-        nc.scalar.copy(out=w_grouped[:], in_=w_raw[:].rearrange("p t q -> p q t"))
+        middle = NQ // 2
+        by_query = w_raw[:].rearrange("p t q -> p q t")
+        nc.scalar.copy(out=w_grouped[:, :middle], in_=by_query[:, :middle])
+        nc.vector.tensor_copy(out=w_grouped[:, middle:], in_=by_query[:, middle:])
         group(BLOCKS - 2)
         quantize(BLOCKS - 2)
         nc.vector.quantize_mx(

from contextlib import ExitStack

import concourse.mybir as mybir
from concourse.masks import make_identity

N, T, DV, NQ = 512, 2048, 512, 128
FLOPS = 2 * N * NQ * DV

P = 128
PACK = 4
BLOCKS = DV // P

F32 = mybir.dt.float32
BF16 = mybir.dt.bfloat16
U32 = mybir.dt.uint32
U16 = mybir.dt.uint16
U8 = mybir.dt.uint8
E4M3X4 = mybir.dt.float8_e4m3fn_x4
E5M2X4 = mybir.dt.float8_e5m2_x4


def tile_attend_spmm_kernel(tc, wT, vT, offs, out):
    nc = tc.nc
    with ExitStack() as ctx:
        hold = ctx.enter_context(tc.tile_pool(name="hold", bufs=1))
        psum = ctx.enter_context(tc.psum_pool(name="psum", bufs=1))

        ident = hold.tile([P, P], F32, name="ident")
        make_identity(nc, ident[:])

        offsets = hold.tile([P, N // 16], U16, name="offsets")
        pool_v = [hold.tile([P, T], F32, name=f"pool_v{b}", tag=f"pool{b}", align_bytes=64) for b in range(BLOCKS)]
        w_raw = hold.tile([P, PACK, NQ], F32, name="w_raw", align_bytes=64)

        for b in range(BLOCKS):
            nc.sync.dma_start(out=pool_v[b][:], in_=vT[b * P:(b + 1) * P, :])
            if b == 0:
                nc.sync.dma_start(offsets[:], offs)
        nc.sync.dma_start(out=w_raw[:], in_=wT.flatten_outer_dims().rearrange("(p t) q -> p t q", t=PACK))

        v_codes = hold.tile([P, DV], U32, name="v_codes", align_bytes=64)
        v_scales = hold.tile([P, DV], U8, name="v_scales", align_bytes=64)
        w_codes = hold.tile([P, NQ], U32, name="w_codes", align_bytes=64)
        w_scales = hold.tile([P, NQ], U8, name="w_scales", align_bytes=64)

        turned = {}
        grouped = {}

        def gather(b):
            picked = hold.tile([P, 2, P, 2], BF16, name=f"picked{b}", align_bytes=64)
            nc.vector.tensor_copy(picked[:].rearrange("d u p e -> d p u e"), pool_v[b][:].indirect(offsets[:]))
            words = picked[:].rearrange("d u p e -> d (u p e)").bitcast(F32)
            turned[b] = psum.tile([P, 2, P], F32, name=f"turned{b}")
            for u in range(2):
                nc.tensor.transpose(turned[b][:, u, :], words[:, u * P:(u + 1) * P], ident[:])

        def group(b):
            g = hold.tile([P, P, PACK], BF16, name=f"grouped{b}", tag=f"pool{b + 1}", align_bytes=64)
            nc.scalar.copy(out=g[:].bitcast(F32), in_=turned[b][:].rearrange("p u r -> p r u"))
            grouped[b] = g

        def quantize(b):
            cols = slice(b * P, (b + 1) * P)
            nc.vector.quantize_mx(
                out=v_codes[:, cols].bitcast(E4M3X4),
                scales=v_scales[:, cols],
                in_=grouped[b][:].rearrange("p r t -> p (r t)"),
            )

        gather(0)
        for b in range(1, BLOCKS - 1):
            gather(b)
            group(b - 1)
            quantize(b - 1)
        gather(BLOCKS - 1)
        w_grouped = hold.tile([P, NQ, PACK], BF16, name="w_grouped", align_bytes=64)
        middle = NQ // 2
        by_query = w_raw[:].rearrange("p t q -> p q t")
        nc.scalar.copy(out=w_grouped[:, :middle], in_=by_query[:, :middle])
        nc.vector.tensor_copy(out=w_grouped[:, middle:], in_=by_query[:, middle:])
        group(BLOCKS - 2)
        quantize(BLOCKS - 2)
        nc.vector.quantize_mx(
            out=w_codes[:].bitcast(E5M2X4),
            scales=w_scales[:],
            in_=w_grouped[:].rearrange("p q t -> p (q t)"),
        )
        group(BLOCKS - 1)
        quantize(BLOCKS - 1)

        acc = psum.tile([NQ, DV], F32, name="acc")
        nc.tensor.matmul_mx(
            out=acc[:],
            lhsT=w_codes[:].bitcast(E5M2X4),
            lhsT_scale=w_scales[:],
            rhs=v_codes[:].bitcast(E4M3X4),
            rhs_scale=v_scales[:],
            start=True,
            stop=True,
        )
        result = out.flatten_outer_dims()
        half = DV // 2
        left = hold.tile([NQ, half], F32, name="left")
        right = hold.tile([NQ, half], F32, name="right")
        nc.vector.tensor_copy(left[:], acc[:, 0:half])
        nc.sync.dma_start(out=result[:, 0:half], in_=left[:])
        nc.scalar.copy(out=right[:], in_=acc[:, half:DV])
        nc.scalar.dma_start(out=result[:, half:DV], in_=right[:])
